import numpy as np
import ml_dtypes


def mxq(x, axis, fmt="e4m3"):
    dtype, down = {"e4m3": (ml_dtypes.float8_e4m3fn, 7), "e5m2": (ml_dtypes.float8_e5m2, 14)}[fmt]
    v = np.moveaxis(np.asarray(x, np.float32).astype(ml_dtypes.bfloat16).astype(np.float64), axis, -1)
    blocks = v.reshape(v.shape[:-1] + (-1, 32))
    amax = np.abs(blocks).max(-1, keepdims=True)
    byte = np.maximum(np.where(amax > 0, np.frexp(amax)[1] - 1 + 127, 0) - down, 1)
    scale = np.exp2(byte - 127.0)
    codes = (blocks / scale).astype(np.float32).astype(dtype).astype(np.float64)
    return np.moveaxis((codes * scale).reshape(v.shape), -1, axis)


WIDE = False


def mx_kscale(k, group=512):
    if not WIDE:
        return np.ones(k)
    levels = np.array([18, -18])
    if group != 512:
        return np.exp2(np.random.permutation(np.resize(levels, k // group))).repeat(group)
    if k % 512:
        return np.exp2(np.random.permutation(np.resize(levels, k // 32))).repeat(32)
    a = np.empty((k // 512, 16))
    for p in range(k // 512):
        a[p, :8] = np.random.permutation(np.resize(levels, 8))
        for g in range(8):
            far = levels[np.abs(levels - a[p, g]) >= 10]
            a[p, g + 8] = far[np.random.randint(len(far))]
    return np.exp2(a.ravel()).repeat(32)


def f64(x):
    return np.asarray(x).astype(np.float64)


def gelu(v):
    return 0.5 * v * (1.0 + np.tanh(0.7978845608028654 * (v + 0.044715 * v ** 3)))


def bf(x):
    return np.asarray(x, np.float32).astype(ml_dtypes.bfloat16)


def planes(Y):
    r, m = Y.shape
    b = f64(bf(Y)).reshape(r // 32, 32, m)
    amax = np.abs(b).max(1)
    byte = np.clip(np.where(amax > 0, np.frexp(amax)[1] - 1 + 127 - 7, 1), 1, 254)
    codes = (b * np.exp2(127.0 - byte)[:, None, :]).reshape(r, m).astype(np.float32).astype(ml_dtypes.float8_e4m3fn).view(np.uint8)
    words = codes.reshape(r // 512, 128, 4, m).transpose(0, 1, 3, 2)
    return np.ascontiguousarray(words), np.ascontiguousarray(byte.astype(np.uint8).reshape(r // 512, 16, m))


G, D, M, N, L = 4, 128, 128, 512, 1024


def setup_inputs():
    n = np.random.standard_normal
    s_d = mx_kscale(D, 0)
    return {
        "x": (n((G, D, L)) * s_d[:, None]).astype(np.float32),
        "w0": (n((G, D, M)) / np.sqrt(5 * D) / s_d[:, None]).astype(np.float32),
        "w1": (n((G, D, M)) / np.sqrt(5 * D) / s_d[:, None]).astype(np.float32),
        "w2": (n((G, D, M)) / np.sqrt(5 * D) / s_d[:, None]).astype(np.float32),
        "w3": (n((G, D, M)) / np.sqrt(5 * D) / s_d[:, None]).astype(np.float32),
        "w4": (n((G, D, M)) / np.sqrt(5 * D) / s_d[:, None]).astype(np.float32),
        "r": (n((G, M, N))).astype(np.float32),
    }


def reference(x, w0, w1, w2, w3, w4, r):
    w0q = mxq(f64(w0), 1, "e4m3")
    xq = mxq(f64(x), 1, "e4m3")
    w1q = mxq(f64(w1), 1, "e4m3")
    w2q = mxq(f64(w2), 1, "e4m3")
    w3q = mxq(f64(w3), 1, "e4m3")
    w4q = mxq(f64(w4), 1, "e4m3")
    z = (w0q.transpose(0, 2, 1) @ xq[..., :512]) + (w1q.transpose(0, 2, 1) @ xq[..., 128 : 640]) + (w2q.transpose(0, 2, 1) @ xq[..., 256 : 768]) + (w3q.transpose(0, 2, 1) @ xq[..., 384 : 896]) + (w4q.transpose(0, 2, 1) @ xq[..., 512 : 1024])
    y = gelu(z) + f64(r)
    Y = y.reshape(G * M, N)
    words, scales = planes(Y)
    return Y, words, scales

from contextlib import ExitStack

import concourse.mybir as mybir

G, D, M, N, L = 4, 128, 128, 512, 1024
TAPS = 5
FLOPS = 2 * G * D * M * N * TAPS

F32 = mybir.dt.float32
BF16 = mybir.dt.bfloat16
I32 = mybir.dt.int32
U32 = mybir.dt.uint32
U8 = mybir.dt.uint8
FP8X4 = mybir.dt.float8_e4m3fn_x4
GELU = mybir.ActivationFunctionType.Gelu_apprx_tanh
ADD = mybir.AluOpType.add

P = 128
PACK = 4
ROWS = D // PACK
X_HALF = L // 2
N_PART = 256
X_VECTOR = 352
Y_VECTOR = 160


def interleave(copy, dst, src, c0, c1):
    copy(
        out=dst[:, c0:c1, :].rearrange("p (c i) j -> p c j i", i=4),
        in_=src[:, :, c0:c1].rearrange("p j (c i) -> p c j i", i=4),
    )


def quantize(nc, codes, scales, packed):
    nc.vector.quantize_mx(
        out=codes.bitcast(FP8X4), scales=scales, in_=packed[:].rearrange("p c j -> p (c j)")
    )


def tile_rows_pl_conv_res_kernel(tc, x, w0, w1, w2, w3, w4, r, out_0, out_1, out_2):
    nc = tc.nc
    weights = [w0, w1, w2, w3, w4]
    parts = N // N_PART
    on_vector = nc.vector.tensor_copy
    on_scalar = nc.scalar.copy

    with ExitStack() as ctx:
        pool = ctx.enter_context(tc.tile_pool(name="sbuf", bufs=1))
        psum = ctx.enter_context(tc.psum_pool(name="psum", bufs=1))
        ctx.enter_context(tc.manual_schedule())

        x_rows = x.rearrange("g (p j) l -> (g p) j l", j=PACK)
        x_raw = [pool.tile([P, PACK, X_HALF], F32, name="x_raw%d" % h) for h in range(2)]
        w_raw = [pool.tile([P, PACK, M], F32, name="w_raw%d" % t) for t in range(TAPS)]
        x_bf = [pool.tile([P, X_HALF, PACK], BF16, name="x_bf%d" % h, align_bytes=64) for h in range(2)]
        w_bf = [pool.tile([P, M, PACK], BF16, name="w_bf%d" % t, align_bytes=64) for t in range(TAPS)]
        x_codes = pool.tile([P, L], U32, align_bytes=64)
        x_scales = pool.tile([P, L], U8, align_bytes=64)
        w_codes = [pool.tile([P, M], U32, name="w_codes%d" % t, align_bytes=64) for t in range(TAPS)]
        w_scales = [pool.tile([P, M], U8, name="w_scales%d" % t, align_bytes=64) for t in range(TAPS)]
        res = pool.tile([P, G, N], F32)
        act = pool.tile([P, G, N], F32)
        y = pool.tile([P, G, N], F32)
        y_bf = [[pool.tile([P, N_PART], BF16, name="y_bf%d_%d" % (h, g)) for g in range(G)] for h in range(parts)]
        y_rows = [pool.tile([P, PACK, N_PART], BF16, name="y_rows%d" % h) for h in range(parts)]
        y_packed = [pool.tile([P, N_PART, PACK], BF16, name="y_packed%d" % h, align_bytes=64) for h in range(parts)]
        y_codes = pool.tile([P, N], U32, align_bytes=64)
        y_scales = pool.tile([P, N], U8, align_bytes=64)
        warm = pool.tile([P, 8], F32)
        z = [psum.tile([P, N], F32, name="z%d" % g) for g in range(G)]

        def load_w(t):
            nc.sync.dma_start(out=w_raw[t][:], in_=weights[t].rearrange("g (p j) m -> (g p) j m", j=PACK))

        load_w(0)
        for h in range(2):
            nc.sync.dma_start(out=x_raw[h][:], in_=x_rows[:, :, h * X_HALF : (h + 1) * X_HALF])
        for t in range(1, TAPS):
            load_w(t)
        nc.sync.dma_start(out=res[:], in_=r.rearrange("g m n -> m g n"))

        nc.vector.memset(warm[:, 0:4], 0.0)
        nc.scalar.activation(out=warm[:, 4:8], in_=warm[:, 0:4], func=GELU)

        def quantize_w(t):
            quantize(nc, w_codes[t][:], w_scales[t][:], w_bf[t])

        def multiply(t):
            cols = slice(M * t, M * t + N)
            for g in range(G):
                rows = slice(ROWS * g, ROWS * (g + 1))
                nc.tensor.matmul_mx(
                    out=z[g][:],
                    lhsT=w_codes[t][rows, :].bitcast(FP8X4),
                    lhsT_scale=w_scales[t][rows, :],
                    rhs=x_codes[rows, cols].bitcast(FP8X4),
                    rhs_scale=x_scales[rows, cols],
                    start=(t == 0),
                    stop=(t == TAPS - 1),
                )

        interleave(on_scalar, w_bf[0], w_raw[0], 0, M)
        quantize_w(0)
        for h in range(2):
            cols = slice(h * X_HALF, (h + 1) * X_HALF)
            interleave(on_vector, x_bf[h], x_raw[h], 0, X_VECTOR)
            interleave(on_scalar, x_bf[h], x_raw[h], X_VECTOR, X_HALF)
            quantize(nc, x_codes[:, cols], x_scales[:, cols], x_bf[h])
            if h == 0:
                multiply(0)
        for t in (1, 2):
            interleave(on_scalar, w_bf[t], w_raw[t], 0, M)
            quantize_w(t)
            multiply(t)
        interleave(on_scalar, w_bf[3], w_raw[3], 0, M)
        interleave(on_vector, w_bf[4], w_raw[4], 0, M)
        for t in (3, 4):
            quantize_w(t)
            multiply(t)

        for h in range(parts):
            cols = slice(h * N_PART, (h + 1) * N_PART)
            for g in range(G):
                nc.scalar.activation(out=act[:, g, cols], in_=z[g][:, cols], func=GELU)
                nc.vector.tensor_tensor(out=y_bf[h][g][:], in0=act[:, g, cols], in1=res[:, g, cols], op=ADD)
                nc.sync.dma_start(out=y_rows[h][ROWS * g : ROWS * (g + 1), :, :], in_=y_bf[h][g][:])

        y_out = out_0.rearrange("(g m) n -> m g n", g=G)
        for g0 in range(0, G, 2):
            pair = slice(g0, g0 + 2)
            nc.vector.tensor_tensor(out=y[:, pair, :], in0=act[:, pair, :], in1=res[:, pair, :], op=ADD)
            nc.sync.dma_start(out=y_out[:, pair, :], in_=y[:, pair, :])

        words_out = out_1.rearrange("s p n u -> p (s n u)").bitcast(I32)
        interleave(on_scalar, y_packed[0], y_rows[0], 0, N_PART)
        for h in range(parts):
            cols = slice(h * N_PART, (h + 1) * N_PART)
            if h == 1:
                interleave(on_scalar, y_packed[h], y_rows[h], Y_VECTOR, N_PART)
                interleave(on_vector, y_packed[h], y_rows[h], 0, Y_VECTOR)
            quantize(nc, y_codes[:, cols], y_scales[:, cols], y_packed[h])
            nc.sync.dma_start(out=words_out[:, cols], in_=y_codes[:, cols].bitcast(I32))
        for q in range(G):
            queue = nc.sync if q % 2 == 0 else nc.scalar
            queue.dma_start(
                out=out_2[0, 4 * q : 4 * q + 4, :].bitcast(I32),
                in_=y_scales[ROWS * q : ROWS * q + 4, :].bitcast(I32),
            )
